import numpy as np
CORES = [4,12,20,28,44,60,76,84,92,108,116,124]
N = 12
TK = 512
D = 128 * N
EPS = 0.01
def setup_inputs(rng):
    return {"x": rng.standard_normal((N, 128, TK), dtype=np.float32) * (0.5 + np.abs(rng.standard_normal((1, 1, TK), dtype=np.float32))), "v": rng.standard_normal((N, 128, TK), dtype=np.float32) * (0.5 + np.abs(rng.standard_normal((1, 1, TK), dtype=np.float32)))}
def setup_inputs_big(rng):
    d = setup_inputs(rng)
    for k in ("x", "v"): d[k] = (d[k].astype(np.float32) * 1024.0).astype(d[k].dtype)
    return d
def setup_inputs_small(rng):
    d = setup_inputs(rng)
    for k in ("x",): d[k] = (d[k].astype(np.float32) * (1 / 1024.0)).astype(d[k].dtype)
    return d
def setup_inputs_apart(rng):
    d = setup_inputs(rng)
    f = (10.0 ** rng.permutation(np.linspace(-1.5, 1.5, N))).astype(np.float32).reshape(N, 1, 1)
    for k in ("x", "v"): d[k] = (d[k].astype(np.float32) * f).astype(d[k].dtype)
    return d
def setup_inputs_mixed(rng):
    d = setup_inputs(rng)
    for k in ("x", "v"):
        f = (10.0 ** rng.uniform(-3, 3, (1, 1, TK))).astype(np.float32); shape = rng.integers(3, size=(1, 1, TK))
        x = d[k].astype(np.float32)
        m = x.mean(axis=(0, 1), keepdims=True); level = m + np.sign(x - m) * np.abs(x - m).mean(axis=(0, 1), keepdims=True) * rng.uniform(0.9, 1.1, x.shape).astype(np.float32)
        other = x * np.where(rng.random(x.shape) < 0.5, 0.1, 1.0).astype(np.float32)
        d[k] = (np.where(shape == 1, level, np.where(shape == 2, other, x)) * f).astype(d[k].dtype)
    return d
def reference(x, v):
    X, V = x.astype(np.float64), v.astype(np.float64)
    n = X / np.sqrt((X ** 2).sum(axis=(0, 1)) / D + EPS)
    Z = n + V
    return {"y": (Z / np.sqrt((Z ** 2).sum(axis=(0, 1)) / D + EPS)).astype(np.float32)}

@@ -1,0 +1,298 @@
+import math
+from concourse.bass import DstId, RemoteDMATransfer
+from concourse.mybir import AluOpType, AxisListType, ActivationFunctionType
+
+N = 12
+TK = 512
+D = 128 * N
+EPS = 0.01
+W = 12
+PER_HELPER = 2
+
+SCRATCH = {
+    "xs": ("sbuf", [128, TK], "float32"),
+    "vs": ("sbuf", [128, TK], "float32"),
+    "xx": ("sbuf", [128, TK], "float32"),
+    "xv": ("sbuf", [128, TK], "float32"),
+    "vv": ("sbuf", [128, TK], "float32"),
+    "cst": ("sbuf", [128, 4], "float32"),
+    "ones": ("sbuf", [128, 128], "float32"),
+    "ident": ("sbuf", [128, 128], "float32"),
+    "erow": ("sbuf", [128, W], "float32"),
+    "land": ("sbuf", [128, N * W], "float32"),
+    "hbuf": ("sbuf", [128, W], "float32"),
+    "pass": ("sbuf", [128, 12 * N], "float32"),
+    "S": ("sbuf", [128, 12], "float32"),
+    "sm": ("sbuf", [128, 96], "float32"),
+    "t1": ("sbuf", [128, TK], "float32"),
+    "zT": ("sbuf", [128, TK], "float32"),
+    "dg": ("sbuf", [128, TK], "float32"),
+    "ys": ("sbuf", [128, TK], "float32"),
+    "ps_stat": ("psum", [128, 512], "float32"),
+    "ps_xT": ("psum", [128, 512], "float32"),
+    "ps_vT": ("psum", [128, 512], "float32"),
+    "ps_y0": ("psum", [128, 512], "float32"),
+    "ps_y1": ("psum", [128, 512], "float32"),
+    "ps_y2": ("psum", [128, 512], "float32"),
+    "ps_y3": ("psum", [128, 512], "float32"),
+    "ps_y4": ("psum", [128, 512], "float32"),
+}
+SEMAPHORES = (["lx0", "lx1", "lv0", "lv1", "mc", "mo", "idn",
+               "me", "pst", "pxT", "pvT", "arr", "sent", "vc", "ssP", "ss1", "ss2", "sSvv",
+               "sW", "sm2", "va", "su2", "st"]
+              + ["%s_%d" % (n, j) for n in ("sxx", "svv", "sxv", "t1", "z", "dg") for j in range(4)]
+              + ["%s_%d" % (n, j) for n in ("py", "cy") for j in range(5)])
+
+
+def _bits(mask):
+    return [b for b in range(16) if (mask >> b) & 1]
+
+
+def _mask(bits):
+    return sum(1 << b for b in bits)
+
+
+def _plan(T, topo):
+    cores = list(T.cores)
+    every = range(topo.CHIPS * topo.CORES_PER_CHIP)
+    plan = []
+    for c in cores:
+        direct = [d for d in cores if d != c and topo.may_write(c, d)]
+        cross = [d for d in cores if d != c and not topo.may_write(c, d)]
+        cand = [k for k in every if topo.chip(k) == topo.chip(c) and T.rank_of(k) is None
+                and all(topo.may_write(k, d) for d in cross)]
+        cand.sort(key=lambda k: (topo.die(k) != topo.die(c), k))
+        nh = min(len(cand), int(math.ceil(len(cross) / PER_HELPER)))
+        helpers = [(cand[i], cross[i::nh]) for i in range(nh)]
+        plan.append((c, direct, helpers))
+    return plan
+
+
+def _dst(topo, core):
+    rid, pid, _se = topo.addr(core)
+    return DstId(rid=rid, pnc=pid)
+
+
+def _helper_program(g, core, T, topo, src_rank, dsts, n_in):
+    eng = _bits(topo.mask(core, dsts[0]))
+    for d in dsts:
+        eng = [b for b in eng if b in _bits(topo.mask(core, d))]
+    slot = T.land[:, src_rank * W:(src_rank + 1) * W]
+    g.wait_ge(T.sem.arr, n_in)
+    g.remote_dma_fused([RemoteDMATransfer(dst_ids=[_dst(topo, d) for d in dsts], dma_engine_mask=_mask(eng),
+                                          remote_sem=T.sem.arr, srcs=[T.hbuf[:]], dsts=[slot for _ in dsts])],
+                       local_sem=T.sem.sent)
+    g.wait_ge(T.sem.sent, len(eng))
+
+
+def rank_program(g, core, T, topo):
+    plan = _plan(T, topo)
+    c0, d0, h0 = plan[0]
+    off = _bits(topo.mask(c0, d0[0]))
+    on_only = [b for b in _bits(topo.mask(c0, h0[0][0])) if b not in off]
+    rank = T.rank_of(core)
+    if rank is None:
+        for r, (c, direct, helpers) in enumerate(plan):
+            for i, (h, dsts) in enumerate(helpers):
+                if h == core:
+                    _helper_program(g, core, T, topo, r, dsts, len(on_only) if i < 2 else len(off))
+        return
+
+    sem = T.sem
+    A = AluOpType
+    F = ActivationFunctionType
+    V, Sc, PE, Sy = g.vector, g.scalar, g.tensor, g.sync
+    blk = [slice(128 * j, 128 * (j + 1)) for j in range(4)]
+    half = [slice(256 * h, 256 * (h + 1)) for h in range(2)]
+    lx, lv = [sem.lx0, sem.lx1], [sem.lv0, sem.lv1]
+    sxx, svv, sxv, t1s, zs, dgs = [[sem["%s_%d" % (n, j)] for j in range(4)]
+                                   for n in ("sxx", "svv", "sxv", "t1", "z", "dg")]
+    pys, cys = [[sem["%s_%d" % (n, j)] for j in range(5)] for n in ("py", "cy")]
+
+    for h in range(2):
+        Sy.dma_start(T.xs[:, half[h]], T.x[:, half[h]]).then_inc(lx[h], 16)
+        Sc.dma_start(T.vs[:, half[h]], T.v[:, half[h]]).then_inc(lv[h], 16)
+
+    V.memset(T.cst[:, 0:1], 1.0 / D).then_inc(sem.mc, 1)
+    V.memset(T.cst[:, 1:2], 2.0 / D).then_inc(sem.mc, 1)
+    V.memset(T.ones[:], 1.0).then_inc(sem.mo, 1)
+    V.memset(T.erow[:, 0:4], EPS / N).then_inc(sem.me, 1)
+    V.memset(T.erow[:, 4:8], 0.0).then_inc(sem.me, 1)
+    V.memset(T.erow[:, 8:12], (1.0 + EPS) / N).then_inc(sem.me, 1)
+    g.wait_ge(sem.mo, 1)
+    g.affine_select(T.ident[:], T.ones[:], [[-1, 128]], A.is_equal, 0.0, 0, 1).then_inc(sem.idn, 1)
+
+    PE.wait_ge(sem.mc, 2)
+    for h in range(2):
+        js = (2 * h, 2 * h + 1)
+        Sc.wait_ge(lx[h], 16)
+        for j in js:
+            Sc.activation(T.xx[:, blk[j]], T.xs[:, blk[j]], F.Square).then_inc(sxx[j], 1)
+        Sc.wait_ge(lv[h], 16)
+        for j in js:
+            Sc.activation(T.vv[:, blk[j]], T.vs[:, blk[j]], F.Square).then_inc(svv[j], 1)
+        V.wait_ge(lx[h], 16)
+        V.wait_ge(lv[h], 16)
+        for j in js:
+            V.tensor_tensor(T.xv[:, blk[j]], T.xs[:, blk[j]], T.vs[:, blk[j]], A.mult).then_inc(sxv[j], 1)
+        for s, buf, ready, cc0 in ((0, T.xx, sxx, 0), (2, T.vv, svv, 0), (1, T.xv, sxv, 1)):
+            for j in js:
+                PE.wait_ge(ready[j], 1)
+                PE.matmul(T.ps_stat[:, 4 * s + j:4 * s + j + 1], buf[:, blk[j]], T.cst[:, cc0:cc0 + 1],
+                          True, True).then_inc(sem.pst, 1)
+
+    nv = [0]
+
+    def step(ins):
+        ins.then_inc(sem.vc, 1)
+        nv[0] += 1
+        return nv[0]
+
+    own = T.land[:, rank * W:(rank + 1) * W]
+    own_xx = T.land[:, rank * W:rank * W + 4]
+    V.wait_ge(sem.pst, 12)
+    V.wait_ge(sem.me, 3)
+    n_own = step(V.tensor_tensor(own, T.ps_stat[:, 0:W], T.erow[:], A.add))
+
+    c, direct, helpers = plan[rank]
+    hs = [h for h, _d in helpers]
+    groups = [(hs[:2], on_only)] + ([(hs[2:], off)] if hs[2:] else [])
+    g.wait_ge(sem.vc, n_own)
+    g.remote_dma_fused([RemoteDMATransfer(dst_ids=[_dst(topo, k) for k in ks], dma_engine_mask=_mask(eng),
+                                          remote_sem=sem.arr, srcs=[own], dsts=[T.hbuf[:] for _ in ks])
+                        for ks, eng in groups], local_sem=sem.sent)
+    g.remote_dma_fused([RemoteDMATransfer(dst_ids=[_dst(topo, k) for k in direct], dma_engine_mask=_mask(off),
+                                          remote_sem=sem.arr, srcs=[own], dsts=[own for _ in direct])],
+                       local_sem=sem.sent)
+    g.wait_ge(sem.sent, sum(len(eng) for _ks, eng in groups) + len(off))
+
+    PE.wait_ge(sem.idn, 1)
+    for h in range(2):
+        PE.wait_ge(lx[h], 16)
+        PE.wait_ge(lv[h], 16)
+    for j in range(4):
+        PE.transpose(T.ps_xT[:, blk[j]], T.xs[:, blk[j]], T.ident[:]).then_inc(sem.pxT, 1)
+    for j in range(4):
+        PE.transpose(T.ps_vT[:, blk[j]], T.vs[:, blk[j]], T.ident[:]).then_inc(sem.pvT, 1)
+
+    names = ("qP", "sP", "sPh", "aPi", "w", "rt", "sq", "ue", "qe", "p", "s1h", "m", "Mp", "tt", "a", "u2", "s2",
+             "q2", "cc")
+    I = dict((n, i) for i, n in enumerate(names))
+
+    def all4(n):
+        return T.sm[:, 4 * I[n]:4 * I[n] + 4]
+
+    def col(n, j):
+        return T.sm[:, 4 * I[n] + j:4 * I[n] + j + 1]
+
+    Sc.wait_ge(sem.vc, n_own)
+    Sc.activation(all4("sP"), own_xx, F.Sqrt).then_inc(sem.ssP, 1)
+    V.wait_ge(sem.vc, n_own)
+    step(V.reciprocal(all4("qP"), own_xx))
+    V.wait_ge(sem.ssP, 1)
+    step(V.tensor_scalar(all4("sPh"), all4("sP"), -0.5, None, A.mult))
+    n_early = step(V.reciprocal(all4("aPi"), all4("sP")))
+    V.wait_ge(sem.vc, n_early)
+
+    n_arr = (N - 1) * len(off)
+    u, Mxv2, T0 = T.S[:, 0:4], T.S[:, 4:8], T.S[:, 8:12]
+
+    def sum_scalar(k, i, out, done, scale):
+        Sc.activation(T["pass"][:, N * i:N * (i + 1)], T.land[:, k::W], F.Copy, scale=scale,
+                      accum_out=out).then_inc(done, 1)
+
+    Sc.wait_ge(sem.arr, n_arr)
+    Sc.wait_ge(sem.vc, n_early)
+    for k in range(4):
+        sum_scalar(k, k, col("w", k), sem.sW, col("aPi", k))
+    V.wait_ge(sem.arr, n_arr)
+    for k in range(4):
+        n_u = step(V.tensor_reduce(T.S[:, k:k + 1], T.land[:, k::W], AxisListType.X, A.add))
+    for k in range(4, 8):
+        step(V.tensor_reduce(T.S[:, k:k + 1], T.land[:, k::W], AxisListType.X, A.add))
+    Sc.wait_ge(sem.vc, n_u)
+    for j in range(4):
+        Sc.activation(col("rt", j), T.S[:, j:j + 1], F.Sqrt, scale=col("qP", j)).then_inc(sem.ss1, 1)
+    for k in range(4):
+        sum_scalar(8 + k, 4 + k, T.S[:, 8 + k:9 + k], sem.sSvv, 1.0)
+
+    V.wait_ge(sem.vc, n_u)
+    n_ue = step(V.tensor_scalar(all4("ue"), u, -1.0 / EPS, None, A.mult))
+    V.wait_ge(sem.sW, 4)
+    n_sq = step(V.reciprocal(all4("sq"), all4("w")))
+    V.wait_ge(sem.vc, n_ue)
+    step(V.reciprocal(all4("qe"), all4("ue")))
+    V.wait_ge(sem.vc, n_sq)
+    V.wait_ge(sem.ss1, 4)
+    step(V.tensor_tensor(all4("p"), all4("rt"), all4("sq"), A.mult))
+    n_p = step(V.tensor_tensor(all4("s1h"), all4("rt"), all4("sPh"), A.mult))
+    V.wait_ge(sem.vc, n_p)
+    for j in (0, 1):
+        n_m = step(V.tensor_scalar(col("m", j), col("s1h", j), col("p", j), 1.5, A.mult, A.add))
+    step(V.tensor_tensor(all4("Mp"), Mxv2, all4("p"), A.mult))
+    V.wait_ge(sem.sSvv, 4)
+    n_tt = step(V.tensor_tensor(all4("tt"), all4("qe"), T0, A.add))
+    Sc.wait_ge(sem.vc, n_p)
+    for j in (2, 3):
+        Sc.activation(col("m", j), col("s1h", j), F.Identity, bias=1.5, scale=col("p", j)).then_inc(sem.sm2, 1)
+    V.wait_ge(sem.vc, n_m)
+    V.wait_ge(sem.sm2, 2)
+    V.tensor_tensor(all4("a"), all4("p"), all4("m"), A.mult).then_inc(sem.va, 1)
+    V.wait_ge(sem.vc, n_tt)
+    for j in (0, 1):
+        n_u2 = step(V.tensor_scalar(col("u2", j), col("Mp", j), col("m", j), col("tt", j), A.mult, A.add))
+    Sc.wait_ge(sem.sm2, 2)
+    Sc.wait_ge(sem.vc, n_tt)
+    for j in (2, 3):
+        Sc.activation(col("u2", j), col("Mp", j), F.Identity, bias=col("tt", j),
+                      scale=col("m", j)).then_inc(sem.su2, 1)
+    V.wait_ge(sem.vc, n_u2)
+    V.wait_ge(sem.su2, 2)
+    n_q2 = step(V.reciprocal(all4("q2"), all4("u2")))
+
+    def scale_x(j):
+        Sc.activation(T.t1[:, blk[j]], T.ps_xT[:, blk[j]], F.Copy, scale=col("a", j)).then_inc(t1s[j], 1)
+
+    def add_v(j):
+        V.wait_ge(t1s[j], 1)
+        V.tensor_tensor(T.zT[:, blk[j]], T.t1[:, blk[j]], T.ps_vT[:, blk[j]], A.add).then_inc(zs[j], 1)
+
+    Sc.wait_ge(sem.va, 1)
+    Sc.wait_ge(sem.pxT, 4)
+    scale_x(0)
+    Sc.wait_ge(sem.vc, n_u2)
+    Sc.wait_ge(sem.su2, 2)
+    Sc.activation(all4("s2"), all4("u2"), F.Sqrt).then_inc(sem.ss2, 1)
+    for j in (1, 2, 3):
+        scale_x(j)
+
+    V.wait_ge(sem.pvT, 4)
+    add_v(0)
+
+    V.wait_ge(sem.vc, n_q2)
+    V.wait_ge(sem.ss2, 1)
+    V.wait_ge(sem.idn, 1)
+    V.tensor_scalar(T.dg[:, blk[0]], T.ident[:], col("s2", 0), col("q2", 0), A.mult, A.mult).then_inc(dgs[0], 1)
+    n_c = step(V.tensor_tensor(all4("cc"), all4("s2"), all4("q2"), A.mult))
+    for j in (1, 2, 3):
+        add_v(j)
+    Sc.wait_ge(sem.vc, n_c)
+    Sc.wait_ge(sem.idn, 1)
+    for j in (1, 2, 3):
+        Sc.activation(T.dg[:, blk[j]], T.ident[:], F.Copy, scale=col("cc", j)).then_inc(dgs[j], 1)
+    pieces = [(0, 0, 128, T.ps_y0), (1, 128, 128, T.ps_y1), (2, 256, 128, T.ps_y2),
+              (3, 384, 64, T.ps_y3), (3, 448, 64, T.ps_y4)]
+    for i, (j, t0, n, ps) in enumerate(pieces):
+        PE.wait_ge(zs[j], 1)
+        PE.wait_ge(dgs[j], 1)
+        PE.matmul(ps[:, 0:n], T.zT[:, blk[j]], T.dg[:, t0:t0 + n], True, True).then_inc(pys[i], 1)
+    for i, (j, t0, n, ps) in enumerate(pieces):
+        if i % 2 == 0:
+            V.wait_ge(pys[i], 1)
+            V.tensor_copy(T.ys[:, t0:t0 + n], ps[:, 0:n]).then_inc(cys[i], 1)
+        else:
+            Sc.wait_ge(pys[i], 1)
+            Sc.activation(T.ys[:, t0:t0 + n], ps[:, 0:n], F.Copy).then_inc(cys[i], 1)
+        Sy.wait_ge(cys[i], 1)
+        Sy.dma_start(T.y[:, t0:t0 + n], T.ys[:, t0:t0 + n]).then_inc(sem.st, 16)
+    Sy.wait_ge(sem.st, 16 * len(pieces))

@@ -38,7 +38,7 @@ SCRATCH = {
     "ps_y4": ("psum", [128, 512], "float32"),
 }
 SEMAPHORES = (["lx0", "lx1", "lv0", "lv1", "mc", "mo", "idn",
-               "me", "pst", "pxT", "pvT", "arr", "sent", "vc", "ssP", "ss1", "ss2", "sSvv",
+               "me", "pst", "pstA", "pxT", "pvT", "arr", "sent", "vc", "ssP", "ss1", "ss2", "sSvv",
                "sW", "sm2", "va", "su2", "st"]
               + ["%s_%d" % (n, j) for n in ("sxx", "svv", "sxv", "t1", "z", "dg") for j in range(4)]
               + ["%s_%d" % (n, j) for n in ("py", "cy") for j in range(5)])
@@ -73,16 +73,25 @@ def _dst(topo, core):
     return DstId(rid=rid, pnc=pid)
 
 
-def _helper_program(g, core, T, topo, src_rank, dsts, n_in):
+def _helper_program(g, core, T, topo, src_rank, rank_core, i, nh, dsts, n_in):
     eng = _bits(topo.mask(core, dsts[0]))
     for d in dsts:
         eng = [b for b in eng if b in _bits(topo.mask(core, d))]
+    wd = 128 // nh
+    part = T.ident[:, i * wd:(i + 1) * wd]
+    g.vector.memset(T.ones[:, 0:wd], 1.0).then_inc(T.sem.mo, 1)
+    g.wait_ge(T.sem.mo, 1)
+    g.affine_select(part, T.ones[:, 0:wd], [[-1, wd]], AluOpType.is_equal, 0.0, -i * wd, 1).then_inc(T.sem.me, 1)
+    g.wait_ge(T.sem.me, 1)
+    g.remote_dma_fused([RemoteDMATransfer(dst_ids=[_dst(topo, rank_core)], dma_engine_mask=_mask(eng),
+                                          remote_sem=T.sem.idn, srcs=[part], dsts=[part])],
+                       local_sem=T.sem.sent)
     slot = T.land[:, src_rank * W:(src_rank + 1) * W]
-    g.wait_ge(T.sem.arr, n_in)
+    g.wait_ge(T.sem.arr, 2 * n_in)
     g.remote_dma_fused([RemoteDMATransfer(dst_ids=[_dst(topo, d) for d in dsts], dma_engine_mask=_mask(eng),
                                           remote_sem=T.sem.arr, srcs=[T.hbuf[:]], dsts=[slot for _ in dsts])],
                        local_sem=T.sem.sent)
-    g.wait_ge(T.sem.sent, len(eng))
+    g.wait_ge(T.sem.sent, 2 * len(eng))
 
 
 def rank_program(g, core, T, topo):
@@ -95,7 +104,8 @@ def rank_program(g, core, T, topo):
         for r, (c, direct, helpers) in enumerate(plan):
             for i, (h, dsts) in enumerate(helpers):
                 if h == core:
-                    _helper_program(g, core, T, topo, r, dsts, len(on_only) if i < 2 else len(off))
+                    _helper_program(g, core, T, topo, r, c, i, len(helpers), dsts,
+                                    len(on_only) if i < 2 else len(off))
         return
 
     sem = T.sem
@@ -108,6 +118,8 @@ def rank_program(g, core, T, topo):
     sxx, svv, sxv, t1s, zs, dgs = [[sem["%s_%d" % (n, j)] for j in range(4)]
                                    for n in ("sxx", "svv", "sxv", "t1", "z", "dg")]
     pys, cys = [[sem["%s_%d" % (n, j)] for j in range(5)] for n in ("py", "cy")]
+    c, direct, helpers = plan[rank]
+    n_idn = len(helpers) * len(off)
 
     for h in range(2):
         Sy.dma_start(T.xs[:, half[h]], T.x[:, half[h]]).then_inc(lx[h], 16)
@@ -115,12 +127,9 @@ def rank_program(g, core, T, topo):
 
     V.memset(T.cst[:, 0:1], 1.0 / D).then_inc(sem.mc, 1)
     V.memset(T.cst[:, 1:2], 2.0 / D).then_inc(sem.mc, 1)
-    V.memset(T.ones[:], 1.0).then_inc(sem.mo, 1)
     V.memset(T.erow[:, 0:4], EPS / N).then_inc(sem.me, 1)
     V.memset(T.erow[:, 4:8], 0.0).then_inc(sem.me, 1)
     V.memset(T.erow[:, 8:12], (1.0 + EPS) / N).then_inc(sem.me, 1)
-    g.wait_ge(sem.mo, 1)
-    g.affine_select(T.ident[:], T.ones[:], [[-1, 128]], A.is_equal, 0.0, 0, 1).then_inc(sem.idn, 1)
 
     PE.wait_ge(sem.mc, 2)
     for h in range(2):
@@ -138,8 +147,9 @@ def rank_program(g, core, T, topo):
         for s, buf, ready, cc0 in ((0, T.xx, sxx, 0), (2, T.vv, svv, 0), (1, T.xv, sxv, 1)):
             for j in js:
                 PE.wait_ge(ready[j], 1)
-                PE.matmul(T.ps_stat[:, 4 * s + j:4 * s + j + 1], buf[:, blk[j]], T.cst[:, cc0:cc0 + 1],
-                          True, True).then_inc(sem.pst, 1)
+                ps = T.ps_y4 if s == 0 else T.ps_stat
+                PE.matmul(ps[:, 4 * s + j:4 * s + j + 1], buf[:, blk[j]], T.cst[:, cc0:cc0 + 1],
+                          True, True).then_inc(sem.pstA if s == 0 else sem.pst, 1)
 
     nv = [0]
 
@@ -150,23 +160,29 @@ def rank_program(g, core, T, topo):
 
     own = T.land[:, rank * W:(rank + 1) * W]
     own_xx = T.land[:, rank * W:rank * W + 4]
-    V.wait_ge(sem.pst, 12)
+    own_rest = T.land[:, rank * W + 4:(rank + 1) * W]
+    V.wait_ge(sem.pstA, 4)
     V.wait_ge(sem.me, 3)
-    n_own = step(V.tensor_tensor(own, T.ps_stat[:, 0:W], T.erow[:], A.add))
+    n_ownA = step(V.tensor_tensor(own_xx, T.ps_y4[:, 0:4], T.erow[:, 0:4], A.add))
+    V.wait_ge(sem.pst, 8)
+    n_own = step(V.tensor_tensor(own_rest, T.ps_stat[:, 4:W], T.erow[:, 4:W], A.add))
 
-    c, direct, helpers = plan[rank]
     hs = [h for h, _d in helpers]
     groups = [(hs[:2], on_only)] + ([(hs[2:], off)] if hs[2:] else [])
+    g.wait_ge(sem.vc, n_ownA)
+    g.remote_dma_fused([RemoteDMATransfer(dst_ids=[_dst(topo, k) for k in ks], dma_engine_mask=_mask(eng),
+                                          remote_sem=sem.arr, srcs=[own_xx], dsts=[T.hbuf[:, 0:4] for _ in ks])
+                        for ks, eng in groups], local_sem=sem.sent)
     g.wait_ge(sem.vc, n_own)
     g.remote_dma_fused([RemoteDMATransfer(dst_ids=[_dst(topo, k) for k in ks], dma_engine_mask=_mask(eng),
-                                          remote_sem=sem.arr, srcs=[own], dsts=[T.hbuf[:] for _ in ks])
+                                          remote_sem=sem.arr, srcs=[own_rest], dsts=[T.hbuf[:, 4:W] for _ in ks])
                         for ks, eng in groups], local_sem=sem.sent)
     g.remote_dma_fused([RemoteDMATransfer(dst_ids=[_dst(topo, k) for k in direct], dma_engine_mask=_mask(off),
                                           remote_sem=sem.arr, srcs=[own], dsts=[own for _ in direct])],
                        local_sem=sem.sent)
-    g.wait_ge(sem.sent, sum(len(eng) for _ks, eng in groups) + len(off))
+    g.wait_ge(sem.sent, 2 * sum(len(eng) for _ks, eng in groups) + len(off))
 
-    PE.wait_ge(sem.idn, 1)
+    PE.wait_ge(sem.idn, n_idn)
     for h in range(2):
         PE.wait_ge(lx[h], 16)
         PE.wait_ge(lv[h], 16)
@@ -271,13 +287,13 @@ def rank_program(g, core, T, topo):
 
     V.wait_ge(sem.vc, n_q2)
     V.wait_ge(sem.ss2, 1)
-    V.wait_ge(sem.idn, 1)
+    V.wait_ge(sem.idn, n_idn)
     V.tensor_scalar(T.dg[:, blk[0]], T.ident[:], col("s2", 0), col("q2", 0), A.mult, A.mult).then_inc(dgs[0], 1)
     n_c = step(V.tensor_tensor(all4("cc"), all4("s2"), all4("q2"), A.mult))
     for j in (1, 2, 3):
         add_v(j)
     Sc.wait_ge(sem.vc, n_c)
-    Sc.wait_ge(sem.idn, 1)
+    Sc.wait_ge(sem.idn, n_idn)
     for j in (1, 2, 3):
         Sc.activation(T.dg[:, blk[j]], T.ident[:], F.Copy, scale=col("cc", j)).then_inc(dgs[j], 1)
     pieces = [(0, 0, 128, T.ps_y0), (1, 128, 128, T.ps_y1), (2, 256, 128, T.ps_y2),

import math
from concourse.bass import DstId, RemoteDMATransfer
from concourse.mybir import AluOpType, AxisListType, ActivationFunctionType

N = 12
TK = 512
D = 128 * N
EPS = 0.01
W = 12
PER_HELPER = 2

SCRATCH = {
    "xs": ("sbuf", [128, TK], "float32"),
    "vs": ("sbuf", [128, TK], "float32"),
    "xx": ("sbuf", [128, TK], "float32"),
    "xv": ("sbuf", [128, TK], "float32"),
    "vv": ("sbuf", [128, TK], "float32"),
    "cst": ("sbuf", [128, 4], "float32"),
    "ones": ("sbuf", [128, 128], "float32"),
    "ident": ("sbuf", [128, 128], "float32"),
    "erow": ("sbuf", [128, W], "float32"),
    "land": ("sbuf", [128, N * W], "float32"),
    "hbuf": ("sbuf", [128, W], "float32"),
    "pass": ("sbuf", [128, 12 * N], "float32"),
    "S": ("sbuf", [128, 12], "float32"),
    "sm": ("sbuf", [128, 96], "float32"),
    "t1": ("sbuf", [128, TK], "float32"),
    "zT": ("sbuf", [128, TK], "float32"),
    "dg": ("sbuf", [128, TK], "float32"),
    "ys": ("sbuf", [128, TK], "float32"),
    "ps_stat": ("psum", [128, 512], "float32"),
    "ps_xT": ("psum", [128, 512], "float32"),
    "ps_vT": ("psum", [128, 512], "float32"),
    "ps_y0": ("psum", [128, 512], "float32"),
    "ps_y1": ("psum", [128, 512], "float32"),
    "ps_y2": ("psum", [128, 512], "float32"),
    "ps_y3": ("psum", [128, 512], "float32"),
    "ps_y4": ("psum", [128, 512], "float32"),
}
SEMAPHORES = (["lx0", "lx1", "lv0", "lv1", "mc", "mo", "idn",
               "me", "pst", "pstA", "pxT", "pvT", "arr", "sent", "vc", "ssP", "ss1", "ss2", "sSvv",
               "sW", "sm2", "va", "su2", "st"]
              + ["%s_%d" % (n, j) for n in ("sxx", "svv", "sxv", "t1", "z", "dg") for j in range(4)]
              + ["%s_%d" % (n, j) for n in ("py", "cy") for j in range(5)])


def _bits(mask):
    return [b for b in range(16) if (mask >> b) & 1]


def _mask(bits):
    return sum(1 << b for b in bits)


def _plan(T, topo):
    cores = list(T.cores)
    every = range(topo.CHIPS * topo.CORES_PER_CHIP)
    plan = []
    for c in cores:
        direct = [d for d in cores if d != c and topo.may_write(c, d)]
        cross = [d for d in cores if d != c and not topo.may_write(c, d)]
        cand = [k for k in every if topo.chip(k) == topo.chip(c) and T.rank_of(k) is None
                and all(topo.may_write(k, d) for d in cross)]
        cand.sort(key=lambda k: (topo.die(k) != topo.die(c), k))
        nh = min(len(cand), int(math.ceil(len(cross) / PER_HELPER)))
        helpers = [(cand[i], cross[i::nh]) for i in range(nh)]
        plan.append((c, direct, helpers))
    return plan


def _dst(topo, core):
    rid, pid, _se = topo.addr(core)
    return DstId(rid=rid, pnc=pid)


def _helper_program(g, core, T, topo, src_rank, rank_core, i, nh, dsts, n_in):
    eng = _bits(topo.mask(core, dsts[0]))
    for d in dsts:
        eng = [b for b in eng if b in _bits(topo.mask(core, d))]
    wd = 128 // nh
    part = T.ident[:, i * wd:(i + 1) * wd]
    g.vector.memset(T.ones[:, 0:wd], 1.0).then_inc(T.sem.mo, 1)
    g.wait_ge(T.sem.mo, 1)
    g.affine_select(part, T.ones[:, 0:wd], [[-1, wd]], AluOpType.is_equal, 0.0, -i * wd, 1).then_inc(T.sem.me, 1)
    g.wait_ge(T.sem.me, 1)
    g.remote_dma_fused([RemoteDMATransfer(dst_ids=[_dst(topo, rank_core)], dma_engine_mask=_mask(eng),
                                          remote_sem=T.sem.idn, srcs=[part], dsts=[part])],
                       local_sem=T.sem.sent)
    slot = T.land[:, src_rank * W:(src_rank + 1) * W]
    g.wait_ge(T.sem.arr, 2 * n_in)
    g.remote_dma_fused([RemoteDMATransfer(dst_ids=[_dst(topo, d) for d in dsts], dma_engine_mask=_mask(eng),
                                          remote_sem=T.sem.arr, srcs=[T.hbuf[:]], dsts=[slot for _ in dsts])],
                       local_sem=T.sem.sent)
    g.wait_ge(T.sem.sent, 2 * len(eng))


def rank_program(g, core, T, topo):
    plan = _plan(T, topo)
    c0, d0, h0 = plan[0]
    off = _bits(topo.mask(c0, d0[0]))
    on_only = [b for b in _bits(topo.mask(c0, h0[0][0])) if b not in off]
    rank = T.rank_of(core)
    if rank is None:
        for r, (c, direct, helpers) in enumerate(plan):
            for i, (h, dsts) in enumerate(helpers):
                if h == core:
                    _helper_program(g, core, T, topo, r, c, i, len(helpers), dsts,
                                    len(on_only) if i < 2 else len(off))
        return

    sem = T.sem
    A = AluOpType
    F = ActivationFunctionType
    V, Sc, PE, Sy = g.vector, g.scalar, g.tensor, g.sync
    blk = [slice(128 * j, 128 * (j + 1)) for j in range(4)]
    half = [slice(256 * h, 256 * (h + 1)) for h in range(2)]
    lx, lv = [sem.lx0, sem.lx1], [sem.lv0, sem.lv1]
    sxx, svv, sxv, t1s, zs, dgs = [[sem["%s_%d" % (n, j)] for j in range(4)]
                                   for n in ("sxx", "svv", "sxv", "t1", "z", "dg")]
    pys, cys = [[sem["%s_%d" % (n, j)] for j in range(5)] for n in ("py", "cy")]
    c, direct, helpers = plan[rank]
    n_idn = len(helpers) * len(off)

    for h in range(2):
        Sy.dma_start(T.xs[:, half[h]], T.x[:, half[h]]).then_inc(lx[h], 16)
        Sc.dma_start(T.vs[:, half[h]], T.v[:, half[h]]).then_inc(lv[h], 16)

    V.memset(T.cst[:, 0:1], 1.0 / D).then_inc(sem.mc, 1)
    V.memset(T.cst[:, 1:2], 2.0 / D).then_inc(sem.mc, 1)
    V.memset(T.erow[:, 0:4], EPS / N).then_inc(sem.me, 1)
    V.memset(T.erow[:, 4:8], 0.0).then_inc(sem.me, 1)
    V.memset(T.erow[:, 8:12], (1.0 + EPS) / N).then_inc(sem.me, 1)

    PE.wait_ge(sem.mc, 2)
    for h in range(2):
        js = (2 * h, 2 * h + 1)
        Sc.wait_ge(lx[h], 16)
        for j in js:
            Sc.activation(T.xx[:, blk[j]], T.xs[:, blk[j]], F.Square).then_inc(sxx[j], 1)
        Sc.wait_ge(lv[h], 16)
        for j in js:
            Sc.activation(T.vv[:, blk[j]], T.vs[:, blk[j]], F.Square).then_inc(svv[j], 1)
        V.wait_ge(lx[h], 16)
        V.wait_ge(lv[h], 16)
        for j in js:
            V.tensor_tensor(T.xv[:, blk[j]], T.xs[:, blk[j]], T.vs[:, blk[j]], A.mult).then_inc(sxv[j], 1)
        for s, buf, ready, cc0 in ((0, T.xx, sxx, 0), (2, T.vv, svv, 0), (1, T.xv, sxv, 1)):
            for j in js:
                PE.wait_ge(ready[j], 1)
                ps = T.ps_y4 if s == 0 else T.ps_stat
                PE.matmul(ps[:, 4 * s + j:4 * s + j + 1], buf[:, blk[j]], T.cst[:, cc0:cc0 + 1],
                          True, True).then_inc(sem.pstA if s == 0 else sem.pst, 1)

    nv = [0]

    def step(ins):
        ins.then_inc(sem.vc, 1)
        nv[0] += 1
        return nv[0]

    own = T.land[:, rank * W:(rank + 1) * W]
    own_xx = T.land[:, rank * W:rank * W + 4]
    own_rest = T.land[:, rank * W + 4:(rank + 1) * W]
    V.wait_ge(sem.pstA, 4)
    V.wait_ge(sem.me, 3)
    n_ownA = step(V.tensor_tensor(own_xx, T.ps_y4[:, 0:4], T.erow[:, 0:4], A.add))
    V.wait_ge(sem.pst, 8)
    n_own = step(V.tensor_tensor(own_rest, T.ps_stat[:, 4:W], T.erow[:, 4:W], A.add))

    hs = [h for h, _d in helpers]
    groups = [(hs[:2], on_only)] + ([(hs[2:], off)] if hs[2:] else [])
    g.wait_ge(sem.vc, n_ownA)
    g.remote_dma_fused([RemoteDMATransfer(dst_ids=[_dst(topo, k) for k in ks], dma_engine_mask=_mask(eng),
                                          remote_sem=sem.arr, srcs=[own_xx], dsts=[T.hbuf[:, 0:4] for _ in ks])
                        for ks, eng in groups], local_sem=sem.sent)
    g.wait_ge(sem.vc, n_own)
    g.remote_dma_fused([RemoteDMATransfer(dst_ids=[_dst(topo, k) for k in ks], dma_engine_mask=_mask(eng),
                                          remote_sem=sem.arr, srcs=[own_rest], dsts=[T.hbuf[:, 4:W] for _ in ks])
                        for ks, eng in groups], local_sem=sem.sent)
    g.remote_dma_fused([RemoteDMATransfer(dst_ids=[_dst(topo, k) for k in direct], dma_engine_mask=_mask(off),
                                          remote_sem=sem.arr, srcs=[own], dsts=[own for _ in direct])],
                       local_sem=sem.sent)
    g.wait_ge(sem.sent, 2 * sum(len(eng) for _ks, eng in groups) + len(off))

    PE.wait_ge(sem.idn, n_idn)
    for h in range(2):
        PE.wait_ge(lx[h], 16)
        PE.wait_ge(lv[h], 16)
    for j in range(4):
        PE.transpose(T.ps_xT[:, blk[j]], T.xs[:, blk[j]], T.ident[:]).then_inc(sem.pxT, 1)
    for j in range(4):
        PE.transpose(T.ps_vT[:, blk[j]], T.vs[:, blk[j]], T.ident[:]).then_inc(sem.pvT, 1)

    names = ("qP", "sP", "sPh", "aPi", "w", "rt", "sq", "ue", "qe", "p", "s1h", "m", "Mp", "tt", "a", "u2", "s2",
             "q2", "cc")
    I = dict((n, i) for i, n in enumerate(names))

    def all4(n):
        return T.sm[:, 4 * I[n]:4 * I[n] + 4]

    def col(n, j):
        return T.sm[:, 4 * I[n] + j:4 * I[n] + j + 1]

    Sc.wait_ge(sem.vc, n_own)
    Sc.activation(all4("sP"), own_xx, F.Sqrt).then_inc(sem.ssP, 1)
    V.wait_ge(sem.vc, n_own)
    step(V.reciprocal(all4("qP"), own_xx))
    V.wait_ge(sem.ssP, 1)
    step(V.tensor_scalar(all4("sPh"), all4("sP"), -0.5, None, A.mult))
    n_early = step(V.reciprocal(all4("aPi"), all4("sP")))
    V.wait_ge(sem.vc, n_early)

    n_arr = (N - 1) * len(off)
    u, Mxv2, T0 = T.S[:, 0:4], T.S[:, 4:8], T.S[:, 8:12]

    def sum_scalar(k, i, out, done, scale):
        Sc.activation(T["pass"][:, N * i:N * (i + 1)], T.land[:, k::W], F.Copy, scale=scale,
                      accum_out=out).then_inc(done, 1)

    Sc.wait_ge(sem.arr, n_arr)
    Sc.wait_ge(sem.vc, n_early)
    for k in range(4):
        sum_scalar(k, k, col("w", k), sem.sW, col("aPi", k))
    V.wait_ge(sem.arr, n_arr)
    for k in range(4):
        n_u = step(V.tensor_reduce(T.S[:, k:k + 1], T.land[:, k::W], AxisListType.X, A.add))
    for k in range(4, 8):
        step(V.tensor_reduce(T.S[:, k:k + 1], T.land[:, k::W], AxisListType.X, A.add))
    Sc.wait_ge(sem.vc, n_u)
    for j in range(4):
        Sc.activation(col("rt", j), T.S[:, j:j + 1], F.Sqrt, scale=col("qP", j)).then_inc(sem.ss1, 1)
    for k in range(4):
        sum_scalar(8 + k, 4 + k, T.S[:, 8 + k:9 + k], sem.sSvv, 1.0)

    V.wait_ge(sem.vc, n_u)
    n_ue = step(V.tensor_scalar(all4("ue"), u, -1.0 / EPS, None, A.mult))
    V.wait_ge(sem.sW, 4)
    n_sq = step(V.reciprocal(all4("sq"), all4("w")))
    V.wait_ge(sem.vc, n_ue)
    step(V.reciprocal(all4("qe"), all4("ue")))
    V.wait_ge(sem.vc, n_sq)
    V.wait_ge(sem.ss1, 4)
    step(V.tensor_tensor(all4("p"), all4("rt"), all4("sq"), A.mult))
    n_p = step(V.tensor_tensor(all4("s1h"), all4("rt"), all4("sPh"), A.mult))
    V.wait_ge(sem.vc, n_p)
    for j in (0, 1):
        n_m = step(V.tensor_scalar(col("m", j), col("s1h", j), col("p", j), 1.5, A.mult, A.add))
    step(V.tensor_tensor(all4("Mp"), Mxv2, all4("p"), A.mult))
    V.wait_ge(sem.sSvv, 4)
    n_tt = step(V.tensor_tensor(all4("tt"), all4("qe"), T0, A.add))
    Sc.wait_ge(sem.vc, n_p)
    for j in (2, 3):
        Sc.activation(col("m", j), col("s1h", j), F.Identity, bias=1.5, scale=col("p", j)).then_inc(sem.sm2, 1)
    V.wait_ge(sem.vc, n_m)
    V.wait_ge(sem.sm2, 2)
    V.tensor_tensor(all4("a"), all4("p"), all4("m"), A.mult).then_inc(sem.va, 1)
    V.wait_ge(sem.vc, n_tt)
    for j in (0, 1):
        n_u2 = step(V.tensor_scalar(col("u2", j), col("Mp", j), col("m", j), col("tt", j), A.mult, A.add))
    Sc.wait_ge(sem.sm2, 2)
    Sc.wait_ge(sem.vc, n_tt)
    for j in (2, 3):
        Sc.activation(col("u2", j), col("Mp", j), F.Identity, bias=col("tt", j),
                      scale=col("m", j)).then_inc(sem.su2, 1)
    V.wait_ge(sem.vc, n_u2)
    V.wait_ge(sem.su2, 2)
    n_q2 = step(V.reciprocal(all4("q2"), all4("u2")))

    def scale_x(j):
        Sc.activation(T.t1[:, blk[j]], T.ps_xT[:, blk[j]], F.Copy, scale=col("a", j)).then_inc(t1s[j], 1)

    def add_v(j):
        V.wait_ge(t1s[j], 1)
        V.tensor_tensor(T.zT[:, blk[j]], T.t1[:, blk[j]], T.ps_vT[:, blk[j]], A.add).then_inc(zs[j], 1)

    Sc.wait_ge(sem.va, 1)
    Sc.wait_ge(sem.pxT, 4)
    scale_x(0)
    Sc.wait_ge(sem.vc, n_u2)
    Sc.wait_ge(sem.su2, 2)
    Sc.activation(all4("s2"), all4("u2"), F.Sqrt).then_inc(sem.ss2, 1)
    for j in (1, 2, 3):
        scale_x(j)

    V.wait_ge(sem.pvT, 4)
    add_v(0)

    V.wait_ge(sem.vc, n_q2)
    V.wait_ge(sem.ss2, 1)
    V.wait_ge(sem.idn, n_idn)
    V.tensor_scalar(T.dg[:, blk[0]], T.ident[:], col("s2", 0), col("q2", 0), A.mult, A.mult).then_inc(dgs[0], 1)
    n_c = step(V.tensor_tensor(all4("cc"), all4("s2"), all4("q2"), A.mult))
    for j in (1, 2, 3):
        add_v(j)
    Sc.wait_ge(sem.vc, n_c)
    Sc.wait_ge(sem.idn, n_idn)
    for j in (1, 2, 3):
        Sc.activation(T.dg[:, blk[j]], T.ident[:], F.Copy, scale=col("cc", j)).then_inc(dgs[j], 1)
    pieces = [(0, 0, 128, T.ps_y0), (1, 128, 128, T.ps_y1), (2, 256, 128, T.ps_y2),
              (3, 384, 64, T.ps_y3), (3, 448, 64, T.ps_y4)]
    for i, (j, t0, n, ps) in enumerate(pieces):
        PE.wait_ge(zs[j], 1)
        PE.wait_ge(dgs[j], 1)
        PE.matmul(ps[:, 0:n], T.zT[:, blk[j]], T.dg[:, t0:t0 + n], True, True).then_inc(pys[i], 1)
    for i, (j, t0, n, ps) in enumerate(pieces):
        if i % 2 == 0:
            V.wait_ge(pys[i], 1)
            V.tensor_copy(T.ys[:, t0:t0 + n], ps[:, 0:n]).then_inc(cys[i], 1)
        else:
            Sc.wait_ge(pys[i], 1)
            Sc.activation(T.ys[:, t0:t0 + n], ps[:, 0:n], F.Copy).then_inc(cys[i], 1)
        Sy.wait_ge(cys[i], 1)
        Sy.dma_start(T.y[:, t0:t0 + n], T.ys[:, t0:t0 + n]).then_inc(sem.st, 16)
    Sy.wait_ge(sem.st, 16 * len(pieces))
